import numpy as np
import ml_dtypes


def mxq(x, axis, fmt="e4m3"):
    dtype, down = {"e4m3": (ml_dtypes.float8_e4m3fn, 7), "e5m2": (ml_dtypes.float8_e5m2, 14)}[fmt]
    v = np.moveaxis(np.asarray(x, np.float32).astype(ml_dtypes.bfloat16).astype(np.float64), axis, -1)
    blocks = v.reshape(v.shape[:-1] + (-1, 32))
    amax = np.abs(blocks).max(-1, keepdims=True)
    byte = np.maximum(np.where(amax > 0, np.frexp(amax)[1] - 1 + 127, 0) - down, 1)
    scale = np.exp2(byte - 127.0)
    codes = (blocks / scale).astype(np.float32).astype(dtype).astype(np.float64)
    return np.moveaxis((codes * scale).reshape(v.shape), -1, axis)


WIDE = False


def mx_kscale(k):
    if not WIDE:
        return np.ones(k)
    levels = np.array([10, -10, 5, -5, 0])
    if k % 512:
        return np.exp2(np.random.permutation(np.resize(levels, k // 32))).repeat(32)
    a = np.empty((k // 512, 16))
    for p in range(k // 512):
        a[p, :8] = np.random.permutation(np.resize(levels, 8))
        for g in range(8):
            far = levels[np.abs(levels - a[p, g]) >= 10]
            a[p, g + 8] = far[np.random.randint(len(far))]
    return np.exp2(a.ravel()).repeat(32)


def f64(x):
    return np.asarray(x).astype(np.float64)


def striped(idx):
    return np.tile(np.asarray(idx).reshape(-1, 16).T, (8, 1)).astype(np.uint16)


def unstriped(offs):
    return offs[:16].T.reshape(-1).astype(np.int64)


E2M1 = np.array([0.0, 0.5, 1.0, 1.5, 2.0, 3.0, 4.0, 6.0, -0.0, -0.5, -1.0, -1.5, -2.0, -3.0, -4.0, -6.0])


def pack_weight(w, fmt):
    k, n = w.shape
    w = f64(np.asarray(w, np.float32).astype(ml_dtypes.bfloat16)).reshape(k // 32, 32, n)
    amax = np.abs(w).max(1)
    if fmt == "e4m3":
        byte = np.frexp(amax)[1] - 1 + 127 - 7
    else:
        mant, ex = np.frexp(amax / 6.0)
        byte = np.where(mant > 0.5, ex, ex - 1) + 127
    byte = np.clip(np.where(amax > 0, byte, 1), 1, 254)
    scaled = (w * np.exp2(127.0 - byte)[:, None, :]).reshape(k, n).astype(np.float32)
    by_word = np.ascontiguousarray(scaled.reshape(k // 512, 128, 4, n).transpose(0, 1, 3, 2))
    if fmt == "e4m3":
        words = by_word.astype(ml_dtypes.float8_e4m3fn).view(np.uint8)
    else:
        c = by_word.astype(ml_dtypes.float4_e2m1fn).view(np.uint8) & 0xF
        words = (c[..., 0::2] | (c[..., 1::2] << 4)).reshape(k // 512, 128, 2 * n)
    return np.ascontiguousarray(words), np.ascontiguousarray(byte.astype(np.uint8).reshape(k // 512, 16, n))


def unpack_weight(words, scales, fmt):
    g, _, n = scales.shape
    words = np.ascontiguousarray(words).reshape(g, 128, n, -1)
    if fmt == "e4m3":
        vals = words.view(ml_dtypes.float8_e4m3fn).astype(np.float64)
    else:
        nib = np.empty((g, 128, n, 4), np.uint8)
        nib[..., 0::2] = words & 0xF
        nib[..., 1::2] = words >> 4
        vals = E2M1[nib]
    vals = vals * np.repeat(np.exp2(scales.astype(np.float64) - 127.0), 8, axis=1)[..., None]
    return vals.transpose(0, 1, 3, 2).reshape(g * 512, n)


K, T, I, J, N, Z, S, C, E = 512, 1024, 512, 256, 256, 1024, 1024, 512, 1024


def setup_inputs():
    n = np.random.standard_normal
    idx = np.random.permutation(T)[:I]
    idx2 = np.random.permutation(Z)[:J]
    idx3 = np.random.permutation(Z)[:J]
    idx4 = np.random.permutation(C)[:J]
    idx5 = np.random.permutation(C)[:J]
    idx6 = np.random.permutation(S)[:N]
    idx7 = np.random.permutation(E)[:J]
    fk = mx_kscale(K)
    fi = mx_kscale(I)
    ti = np.ones(T)
    ti[idx] = fi
    xkp = pack_weight(n((K, T)) * 0.3 * fk[:, None] * ti, "e4m3")
    xqp = pack_weight(n((K, Z)) * 0.3 / fk[:, None], "e2m1")
    vsp = pack_weight(n((I, S)) / fi[:, None], "e2m1")
    return {
        "xk_words": xkp[0],
        "xk_scales": xkp[1],
        "xq_words": xqp[0],
        "xq_scales": xqp[1],
        "vs_words": vsp[0],
        "vs_scales": vsp[1],
        "offs": striped(idx),
        "offs2": striped(idx2),
        "offs3": striped(idx3),
        "offs4": striped(idx4),
        "offs5": striped(idx5),
        "offs6": striped(idx6),
        "offs7": striped(idx7),
    }


def reference(xk_words, xk_scales, xq_words, xq_scales, vs_words, vs_scales, offs, offs2, offs3, offs4, offs5, offs6, offs7):
    idx = unstriped(offs)
    idx2 = unstriped(offs2)
    idx3 = unstriped(offs3)
    idx4 = unstriped(offs4)
    idx5 = unstriped(offs5)
    idx6 = unstriped(offs6)
    idx7 = unstriped(offs7)
    xku = unpack_weight(xk_words, xk_scales, "e4m3")
    xqu = unpack_weight(xq_words, xq_scales, "e2m1")
    vsu = unpack_weight(vs_words, vs_scales, "e2m1")
    xkidxg = xku[:, idx]
    xqidx2g = xqu[:, idx2]
    s1 = xkidxg.T @ xqidx2g
    xqidx3g = xqu[:, idx3]
    s2 = xkidxg.T @ xqidx3g
    pw = np.zeros((I, C))
    pw[:, idx4] = s1
    hid = np.abs(pw[:, idx5] - s2)
    vsidx6g = vsu[:, idx6]
    hidq = mxq(hid, 0, "e4m3")
    p = vsidx6g.T @ hidq
    y = np.zeros((N, E))
    y[:, idx7] = p
    return y

@@ -1,0 +1,184 @@
+from contextlib import ExitStack
+
+import concourse.mybir as mybir
+
+K, T, I, J, N, Z, S, C, E = 512, 1024, 512, 256, 256, 1024, 1024, 512, 1024
+FLOPS = 2 * K * I * J * 2 + 2 * I * N * J
+
+F32 = mybir.dt.float32
+BF16 = mybir.dt.bfloat16
+I32 = mybir.dt.int32
+U32 = mybir.dt.uint32
+U16 = mybir.dt.uint16
+U8 = mybir.dt.uint8
+E4M3 = mybir.dt.float8_e4m3fn_x4
+E2M1 = mybir.dt.float4_e2m1fn_x4
+ACT = mybir.ActivationFunctionType
+ALU = mybir.AluOpType
+
+P = 128
+PACK = 4
+HALF = J // 2
+LIST_COLS = HALF // 16
+
+
+def tile_list_contest_twice_board_scattered_kernel(
+    tc, xk_words, xk_scales, xq_words, xq_scales, vs_words, vs_scales,
+    offs, offs2, offs3, offs4, offs5, offs6, offs7, out,
+):
+    nc = tc.nc
+    with ExitStack() as ctx:
+        sb = ctx.enter_context(tc.tile_pool(name="sb", bufs=1))
+        ps = ctx.enter_context(tc.psum_pool(name="ps", bufs=1))
+
+        def load_list(name, src):
+            tile = sb.tile(list(src.shape), U16, name=name)
+            nc.sync.dma_start(tile[:], src)
+            return tile
+
+        def zeroed_plane(name):
+            plane = sb.tile([P, T], U8, name=name)
+            nc.gpsimd.memset(plane[:].bitcast(I32), 0)
+            return plane
+
+        def load_scales(plane, src):
+            rows = src[0].bitcast(I32)
+            for q in range(4):
+                nc.sync.dma_start(plane[32 * q : 32 * q + 4, :].bitcast(I32), rows[4 * q : 4 * q + 4, :])
+
+        def half_of(lst, h):
+            return lst[:, h * LIST_COLS : (h + 1) * LIST_COLS]
+
+        xk_plane = zeroed_plane("xk_plane")
+        xq_plane = zeroed_plane("xq_plane")
+        boards = [sb.tile([P, C], F32, name=f"board{t}") for t in range(PACK)]
+        pages = [sb.tile([P, E], F32, name=f"page{m}") for m in range(N // P)]
+        for t in (0, 3, 1, 2):
+            nc.gpsimd.memset(boards[t][:], 0.0)
+        vs_plane = zeroed_plane("vs_plane")
+        for page in pages:
+            nc.gpsimd.memset(page[:], 0.0)
+
+        xk_tab = sb.tile([P, T], U32, name="xk_tab")
+        xq_tab = sb.tile([P, Z], U16, name="xq_tab")
+        vs_tab = sb.tile([P, S], U16, name="vs_tab")
+
+        l1 = load_list("l1", offs)
+        load_scales(xk_plane, xk_scales)
+        nc.sync.dma_start(xk_tab[:].bitcast(I32), xk_words[0].rearrange("p n t -> p (n t)").bitcast(I32))
+        l2 = load_list("l2", offs2)
+        nc.sync.dma_start(xq_tab[:].bitcast(I32), xq_words[0].bitcast(I32))
+        load_scales(xq_plane, xq_scales)
+        l3 = load_list("l3", offs3)
+        l4 = load_list("l4", offs4)
+        l5 = load_list("l5", offs5)
+        nc.sync.dma_start(vs_tab[:].bitcast(I32), vs_words[0].bitcast(I32))
+        l6 = load_list("l6", offs6)
+        load_scales(vs_plane, vs_scales)
+        l7 = load_list("l7", offs7)
+
+        def gather_packed(name, tab, plane, lst, count, word_dtype):
+            words = sb.tile([P, count], word_dtype, name=name + "_words", align_bytes=64)
+            scales = sb.tile([P, count], U8, name=name + "_scales", align_bytes=64)
+            nc.vector.tensor_copy(words[:], tab[:].indirect(lst[:]))
+            nc.vector.tensor_copy(scales[:], plane[:].indirect(lst[:]))
+            return words, scales
+
+        k_words = sb.tile([P, I], U32, name="k_words", align_bytes=64)
+        k_scales = sb.tile([P, I], U8, name="k_scales", align_bytes=64)
+        nc.vector.tensor_copy(k_scales[:].rearrange("p (t q) -> p q t", t=PACK), xk_plane[:].indirect(l1[:]))
+        nc.vector.tensor_copy(k_words[:].rearrange("p (t q) -> p q t", t=PACK), xk_tab[:].indirect(l1[:]))
+        q1_words, q1_scales = gather_packed("q1", xq_tab, xq_plane, l2, J, U16)
+
+        def scores(dst, t, words, scales, cols):
+            rows = slice(t * P, (t + 1) * P)
+            nc.tensor.matmul_mx(
+                out=dst,
+                lhsT=k_words[:, rows].bitcast(E4M3),
+                lhsT_scale=k_scales[:, rows],
+                rhs=words[:, cols].bitcast(E2M1),
+                rhs_scale=scales[:, cols],
+                start=True,
+                stop=True,
+            )
+
+        s1_banks = [ps.tile([P, J], F32, name=f"s1_bank{t}") for t in range(PACK)]
+        order = (0, 3, 1, 2)
+        for t in order:
+            scores(s1_banks[t][:], t, q1_words, q1_scales, slice(0, J))
+
+        q2_words, q2_scales = gather_packed("q2", xq_tab, xq_plane, l3, J, U16)
+        s2_banks = [ps.tile([P, PACK, HALF], F32, name=f"s2_bank{h}") for h in range(2)]
+        for h in range(2):
+            for t in range(PACK):
+                scores(s2_banks[h][:, t, :], t, q2_words, q2_scales, slice(h * HALF, (h + 1) * HALF))
+
+        def put(on_vector, window, lst, values):
+            if on_vector:
+                nc.vector.tensor_copy(window[:].indirect(lst), values)
+            else:
+                nc.scalar.activation(window[:].indirect(lst), values, ACT.Copy)
+
+        def pick(on_vector, dst, window, lst):
+            if on_vector:
+                nc.vector.tensor_copy(dst, window[:].indirect(lst))
+            else:
+                nc.scalar.activation(dst, window[:].indirect(lst), ACT.Copy)
+
+        def leave_bank(on_vector, dst, bank):
+            if on_vector:
+                nc.vector.tensor_copy(dst, bank)
+            else:
+                nc.scalar.activation(dst, bank, ACT.Copy)
+
+        for t in order:
+            s1 = sb.tile([P, J], F32, name=f"s1_{t}")
+            leave_bank(t == 3, s1[:], s1_banks[t][:])
+            put(t == 3, boards[t], l4[:], s1[:])
+
+        picked = [sb.tile([P, PACK, HALF], F32, name=f"picked{h}") for h in range(2)]
+        for t in (0, 3, 1):
+            for h in range(2):
+                pick(True, picked[h][:, t, :], boards[t], half_of(l5, h))
+        v_words, v_scales = gather_packed("v", vs_tab, vs_plane, l6, N, U16)
+        for h in range(2):
+            pick(h == 0, picked[h][:, 2, :], boards[2], half_of(l5, h))
+
+        diffs = []
+        for h in range(2):
+            diff = sb.tile([P, PACK, HALF], F32, name=f"diff{h}")
+            nc.vector.tensor_tensor(diff[:], picked[h][:], s2_banks[h][:], ALU.subtract)
+            diffs.append(diff)
+
+        hids = []
+        for h in range(2):
+            hid = sb.tile([P, HALF, PACK], BF16, name=f"hid{h}", align_bytes=64)
+            nc.scalar.activation(hid[:], diffs[h][:].rearrange("p t j -> p j t"), ACT.Abs)
+            hids.append(hid)
+
+        for h in range(2):
+            h_words = sb.tile([P, HALF], U32, name=f"h_words{h}", align_bytes=64)
+            h_scales = sb.tile([P, HALF], U8, name=f"h_scales{h}", align_bytes=64)
+            nc.vector.quantize_mx(
+                out=h_words[:].bitcast(E4M3),
+                scales=h_scales[:],
+                in_=hids[h][:].rearrange("p j t -> p (j t)"),
+            )
+            for m in range(N // P):
+                bank = ps.tile([P, HALF], F32, name=f"p_bank{h}{m}", tag=f"s1_bank{2 * h + m}")
+                cols = slice(m * P, (m + 1) * P)
+                nc.tensor.matmul_mx(
+                    out=bank[:],
+                    lhsT=v_words[:, cols].bitcast(E2M1),
+                    lhsT_scale=v_scales[:, cols],
+                    rhs=h_words[:].bitcast(E4M3),
+                    rhs_scale=h_scales[:],
+                    start=True,
+                    stop=True,
+                )
+                res = sb.tile([P, HALF], F32, name=f"res{h}{m}")
+                leave_bank(m == 0, res[:], bank[:])
+                put(m == 0, pages[m], half_of(l7, h), res[:])
+
+        for m in range(N // P):
+            nc.sync.dma_start(out[m * P : (m + 1) * P, :], pages[m][:])

@@ -41,10 +41,10 @@ def tile_list_contest_twice_board_scattered_kernel(
             nc.gpsimd.memset(plane[:].bitcast(I32), 0)
             return plane
 
-        def load_scales(plane, src):
+        def load_scales(plane, src, queues):
             rows = src[0].bitcast(I32)
             for q in range(4):
-                nc.sync.dma_start(plane[32 * q : 32 * q + 4, :].bitcast(I32), rows[4 * q : 4 * q + 4, :])
+                queues[q % len(queues)].dma_start(plane[32 * q : 32 * q + 4, :].bitcast(I32), rows[4 * q : 4 * q + 4, :])
 
         def half_of(lst, h):
             return lst[:, h * LIST_COLS : (h + 1) * LIST_COLS]
@@ -53,7 +53,7 @@ def tile_list_contest_twice_board_scattered_kernel(
         xq_plane = zeroed_plane("xq_plane")
         boards = [sb.tile([P, C], F32, name=f"board{t}") for t in range(PACK)]
         pages = [sb.tile([P, E], F32, name=f"page{m}") for m in range(N // P)]
-        for t in (0, 3, 1, 2):
+        for t in (0, 2, 1, 3):
             nc.gpsimd.memset(boards[t][:], 0.0)
         vs_plane = zeroed_plane("vs_plane")
         for page in pages:
@@ -63,18 +63,18 @@ def tile_list_contest_twice_board_scattered_kernel(
         xq_tab = sb.tile([P, Z], U16, name="xq_tab")
         vs_tab = sb.tile([P, S], U16, name="vs_tab")
 
-        l1 = load_list("l1", offs)
-        load_scales(xk_plane, xk_scales)
-        nc.sync.dma_start(xk_tab[:].bitcast(I32), xk_words[0].rearrange("p n t -> p (n t)").bitcast(I32))
         l2 = load_list("l2", offs2)
         nc.sync.dma_start(xq_tab[:].bitcast(I32), xq_words[0].bitcast(I32))
-        load_scales(xq_plane, xq_scales)
+        l1 = load_list("l1", offs)
+        load_scales(xk_plane, xk_scales, (nc.sync,))
+        nc.sync.dma_start(xk_tab[:].bitcast(I32), xk_words[0].rearrange("p n t -> p (n t)").bitcast(I32))
+        load_scales(xq_plane, xq_scales, (nc.sync,))
         l3 = load_list("l3", offs3)
         l4 = load_list("l4", offs4)
-        l5 = load_list("l5", offs5)
         nc.sync.dma_start(vs_tab[:].bitcast(I32), vs_words[0].bitcast(I32))
+        load_scales(vs_plane, vs_scales, (nc.sync,))
         l6 = load_list("l6", offs6)
-        load_scales(vs_plane, vs_scales)
+        l5 = load_list("l5", offs5)
         l7 = load_list("l7", offs7)
 
         def gather_packed(name, tab, plane, lst, count, word_dtype):
@@ -103,7 +103,7 @@ def tile_list_contest_twice_board_scattered_kernel(
             )
 
         s1_banks = [ps.tile([P, J], F32, name=f"s1_bank{t}") for t in range(PACK)]
-        order = (0, 3, 1, 2)
+        order = (0, 1, 2, 3)
         for t in order:
             scores(s1_banks[t][:], t, q1_words, q1_scales, slice(0, J))
 
@@ -131,21 +131,18 @@ def tile_list_contest_twice_board_scattered_kernel(
             else:
                 nc.scalar.activation(dst, bank, ACT.Copy)
 
+        s1 = [sb.tile([P, J], F32, name=f"s1_{t}") for t in range(PACK)]
         for t in order:
-            s1 = sb.tile([P, J], F32, name=f"s1_{t}")
-            leave_bank(t == 3, s1[:], s1_banks[t][:])
-            put(t == 3, boards[t], l4[:], s1[:])
+            leave_bank(t >= 2, s1[t][:], s1_banks[t][:])
+        for t in order:
+            put(t >= 2, boards[t], l4[:], s1[t][:])
 
         picked = [sb.tile([P, PACK, HALF], F32, name=f"picked{h}") for h in range(2)]
-        for t in (0, 3, 1):
-            for h in range(2):
-                pick(True, picked[h][:, t, :], boards[t], half_of(l5, h))
         v_words, v_scales = gather_packed("v", vs_tab, vs_plane, l6, N, U16)
-        for h in range(2):
-            pick(h == 0, picked[h][:, 2, :], boards[2], half_of(l5, h))
-
         diffs = []
         for h in range(2):
+            for t in order:
+                pick((h, t) == (1, PACK - 1), picked[h][:, t, :], boards[t], half_of(l5, h))
             diff = sb.tile([P, PACK, HALF], F32, name=f"diff{h}")
             nc.vector.tensor_tensor(diff[:], picked[h][:], s2_banks[h][:], ALU.subtract)
             diffs.append(diff)
@@ -153,9 +150,14 @@ def tile_list_contest_twice_board_scattered_kernel(
         hids = []
         for h in range(2):
             hid = sb.tile([P, HALF, PACK], BF16, name=f"hid{h}", align_bytes=64)
-            nc.scalar.activation(hid[:], diffs[h][:].rearrange("p t j -> p j t"), ACT.Abs)
+            nc.scalar.activation(
+                hid[:].rearrange("p (c u) t -> p c t u", u=4),
+                diffs[h][:].rearrange("p t (c u) -> p c t u", u=4),
+                ACT.Abs,
+            )
             hids.append(hid)
 
+        packed = []
         for h in range(2):
             h_words = sb.tile([P, HALF], U32, name=f"h_words{h}", align_bytes=64)
             h_scales = sb.tile([P, HALF], U8, name=f"h_scales{h}", align_bytes=64)
@@ -164,6 +166,10 @@ def tile_list_contest_twice_board_scattered_kernel(
                 scales=h_scales[:],
                 in_=hids[h][:].rearrange("p j t -> p (j t)"),
             )
+            packed.append((h_words, h_scales))
+
+        for h in range(2):
+            h_words, h_scales = packed[h]
             for m in range(N // P):
                 bank = ps.tile([P, HALF], F32, name=f"p_bank{h}{m}", tag=f"s1_bank{2 * h + m}")
                 cols = slice(m * P, (m + 1) * P)
@@ -180,5 +186,5 @@ def tile_list_contest_twice_board_scattered_kernel(
                 leave_bank(m == 0, res[:], bank[:])
                 put(m == 0, pages[m], half_of(l7, h), res[:])
 
-        for m in range(N // P):
-            nc.sync.dma_start(out[m * P : (m + 1) * P, :], pages[m][:])
+        for m, queue in enumerate((nc.sync, nc.scalar)):
+            queue.dma_start(out[m * P : (m + 1) * P, :], pages[m][:])

from contextlib import ExitStack

import concourse.mybir as mybir

K, T, I, J, N, Z, S, C, E = 512, 1024, 512, 256, 256, 1024, 1024, 512, 1024
FLOPS = 2 * K * I * J * 2 + 2 * I * N * J

F32 = mybir.dt.float32
BF16 = mybir.dt.bfloat16
I32 = mybir.dt.int32
U32 = mybir.dt.uint32
U16 = mybir.dt.uint16
U8 = mybir.dt.uint8
E4M3 = mybir.dt.float8_e4m3fn_x4
E2M1 = mybir.dt.float4_e2m1fn_x4
ACT = mybir.ActivationFunctionType
ALU = mybir.AluOpType

P = 128
PACK = 4
HALF = J // 2
LIST_COLS = HALF // 16


def tile_list_contest_twice_board_scattered_kernel(
    tc, xk_words, xk_scales, xq_words, xq_scales, vs_words, vs_scales,
    offs, offs2, offs3, offs4, offs5, offs6, offs7, out,
):
    nc = tc.nc
    with ExitStack() as ctx:
        sb = ctx.enter_context(tc.tile_pool(name="sb", bufs=1))
        ps = ctx.enter_context(tc.psum_pool(name="ps", bufs=1))

        def load_list(name, src):
            tile = sb.tile(list(src.shape), U16, name=name)
            nc.sync.dma_start(tile[:], src)
            return tile

        def zeroed_plane(name):
            plane = sb.tile([P, T], U8, name=name)
            nc.gpsimd.memset(plane[:].bitcast(I32), 0)
            return plane

        def load_scales(plane, src, queues):
            rows = src[0].bitcast(I32)
            for q in range(4):
                queues[q % len(queues)].dma_start(plane[32 * q : 32 * q + 4, :].bitcast(I32), rows[4 * q : 4 * q + 4, :])

        def half_of(lst, h):
            return lst[:, h * LIST_COLS : (h + 1) * LIST_COLS]

        xk_plane = zeroed_plane("xk_plane")
        xq_plane = zeroed_plane("xq_plane")
        boards = [sb.tile([P, C], F32, name=f"board{t}") for t in range(PACK)]
        pages = [sb.tile([P, E], F32, name=f"page{m}") for m in range(N // P)]
        for t in (0, 2, 1, 3):
            nc.gpsimd.memset(boards[t][:], 0.0)
        vs_plane = zeroed_plane("vs_plane")
        for page in pages:
            nc.gpsimd.memset(page[:], 0.0)

        xk_tab = sb.tile([P, T], U32, name="xk_tab")
        xq_tab = sb.tile([P, Z], U16, name="xq_tab")
        vs_tab = sb.tile([P, S], U16, name="vs_tab")

        l2 = load_list("l2", offs2)
        nc.sync.dma_start(xq_tab[:].bitcast(I32), xq_words[0].bitcast(I32))
        l1 = load_list("l1", offs)
        load_scales(xk_plane, xk_scales, (nc.sync,))
        nc.sync.dma_start(xk_tab[:].bitcast(I32), xk_words[0].rearrange("p n t -> p (n t)").bitcast(I32))
        load_scales(xq_plane, xq_scales, (nc.sync,))
        l3 = load_list("l3", offs3)
        l4 = load_list("l4", offs4)
        nc.sync.dma_start(vs_tab[:].bitcast(I32), vs_words[0].bitcast(I32))
        load_scales(vs_plane, vs_scales, (nc.sync,))
        l6 = load_list("l6", offs6)
        l5 = load_list("l5", offs5)
        l7 = load_list("l7", offs7)

        def gather_packed(name, tab, plane, lst, count, word_dtype):
            words = sb.tile([P, count], word_dtype, name=name + "_words", align_bytes=64)
            scales = sb.tile([P, count], U8, name=name + "_scales", align_bytes=64)
            nc.vector.tensor_copy(words[:], tab[:].indirect(lst[:]))
            nc.vector.tensor_copy(scales[:], plane[:].indirect(lst[:]))
            return words, scales

        k_words = sb.tile([P, I], U32, name="k_words", align_bytes=64)
        k_scales = sb.tile([P, I], U8, name="k_scales", align_bytes=64)
        nc.vector.tensor_copy(k_scales[:].rearrange("p (t q) -> p q t", t=PACK), xk_plane[:].indirect(l1[:]))
        nc.vector.tensor_copy(k_words[:].rearrange("p (t q) -> p q t", t=PACK), xk_tab[:].indirect(l1[:]))
        q1_words, q1_scales = gather_packed("q1", xq_tab, xq_plane, l2, J, U16)

        def scores(dst, t, words, scales, cols):
            rows = slice(t * P, (t + 1) * P)
            nc.tensor.matmul_mx(
                out=dst,
                lhsT=k_words[:, rows].bitcast(E4M3),
                lhsT_scale=k_scales[:, rows],
                rhs=words[:, cols].bitcast(E2M1),
                rhs_scale=scales[:, cols],
                start=True,
                stop=True,
            )

        s1_banks = [ps.tile([P, J], F32, name=f"s1_bank{t}") for t in range(PACK)]
        order = (0, 1, 2, 3)
        for t in order:
            scores(s1_banks[t][:], t, q1_words, q1_scales, slice(0, J))

        q2_words, q2_scales = gather_packed("q2", xq_tab, xq_plane, l3, J, U16)
        s2_banks = [ps.tile([P, PACK, HALF], F32, name=f"s2_bank{h}") for h in range(2)]
        for h in range(2):
            for t in range(PACK):
                scores(s2_banks[h][:, t, :], t, q2_words, q2_scales, slice(h * HALF, (h + 1) * HALF))

        def put(on_vector, window, lst, values):
            if on_vector:
                nc.vector.tensor_copy(window[:].indirect(lst), values)
            else:
                nc.scalar.activation(window[:].indirect(lst), values, ACT.Copy)

        def pick(on_vector, dst, window, lst):
            if on_vector:
                nc.vector.tensor_copy(dst, window[:].indirect(lst))
            else:
                nc.scalar.activation(dst, window[:].indirect(lst), ACT.Copy)

        def leave_bank(on_vector, dst, bank):
            if on_vector:
                nc.vector.tensor_copy(dst, bank)
            else:
                nc.scalar.activation(dst, bank, ACT.Copy)

        s1 = [sb.tile([P, J], F32, name=f"s1_{t}") for t in range(PACK)]
        for t in order:
            leave_bank(t >= 2, s1[t][:], s1_banks[t][:])
        for t in order:
            put(t >= 2, boards[t], l4[:], s1[t][:])

        picked = [sb.tile([P, PACK, HALF], F32, name=f"picked{h}") for h in range(2)]
        v_words, v_scales = gather_packed("v", vs_tab, vs_plane, l6, N, U16)
        diffs = []
        for h in range(2):
            for t in order:
                pick((h, t) == (1, PACK - 1), picked[h][:, t, :], boards[t], half_of(l5, h))
            diff = sb.tile([P, PACK, HALF], F32, name=f"diff{h}")
            nc.vector.tensor_tensor(diff[:], picked[h][:], s2_banks[h][:], ALU.subtract)
            diffs.append(diff)

        hids = []
        for h in range(2):
            hid = sb.tile([P, HALF, PACK], BF16, name=f"hid{h}", align_bytes=64)
            nc.scalar.activation(
                hid[:].rearrange("p (c u) t -> p c t u", u=4),
                diffs[h][:].rearrange("p t (c u) -> p c t u", u=4),
                ACT.Abs,
            )
            hids.append(hid)

        packed = []
        for h in range(2):
            h_words = sb.tile([P, HALF], U32, name=f"h_words{h}", align_bytes=64)
            h_scales = sb.tile([P, HALF], U8, name=f"h_scales{h}", align_bytes=64)
            nc.vector.quantize_mx(
                out=h_words[:].bitcast(E4M3),
                scales=h_scales[:],
                in_=hids[h][:].rearrange("p j t -> p (j t)"),
            )
            packed.append((h_words, h_scales))

        for h in range(2):
            h_words, h_scales = packed[h]
            for m in range(N // P):
                bank = ps.tile([P, HALF], F32, name=f"p_bank{h}{m}", tag=f"s1_bank{2 * h + m}")
                cols = slice(m * P, (m + 1) * P)
                nc.tensor.matmul_mx(
                    out=bank[:],
                    lhsT=v_words[:, cols].bitcast(E2M1),
                    lhsT_scale=v_scales[:, cols],
                    rhs=h_words[:].bitcast(E4M3),
                    rhs_scale=h_scales[:],
                    start=True,
                    stop=True,
                )
                res = sb.tile([P, HALF], F32, name=f"res{h}{m}")
                leave_bank(m == 0, res[:], bank[:])
                put(m == 0, pages[m], half_of(l7, h), res[:])

        for m, queue in enumerate((nc.sync, nc.scalar)):
            queue.dma_start(out[m * P : (m + 1) * P, :], pages[m][:])
